import numpy as np
import ml_dtypes


def mxq(x, axis, fmt="e4m3"):
    dtype, down = {"e4m3": (ml_dtypes.float8_e4m3fn, 7), "e5m2": (ml_dtypes.float8_e5m2, 14)}[fmt]
    v = np.moveaxis(np.asarray(x, np.float32).astype(ml_dtypes.bfloat16).astype(np.float64), axis, -1)
    blocks = v.reshape(v.shape[:-1] + (-1, 32))
    amax = np.abs(blocks).max(-1, keepdims=True)
    byte = np.maximum(np.where(amax > 0, np.frexp(amax)[1] - 1 + 127, 0) - down, 1)
    scale = np.exp2(byte - 127.0)
    codes = (blocks / scale).astype(np.float32).astype(dtype).astype(np.float64)
    return np.moveaxis((codes * scale).reshape(v.shape), -1, axis)


WIDE = False


def mx_kscale(k):
    if not WIDE:
        return np.ones(k)
    levels = np.array([10, -10, 5, -5, 0])
    if k % 512:
        return np.exp2(np.random.permutation(np.resize(levels, k // 32))).repeat(32)
    a = np.empty((k // 512, 16))
    for p in range(k // 512):
        a[p, :8] = np.random.permutation(np.resize(levels, 8))
        for g in range(8):
            far = levels[np.abs(levels - a[p, g]) >= 10]
            a[p, g + 8] = far[np.random.randint(len(far))]
    return np.exp2(a.ravel()).repeat(32)


BF16 = ml_dtypes.bfloat16


def bf(x):
    return np.asarray(x, np.float32).astype(BF16)


def f64(x):
    return np.asarray(x).astype(np.float64)


E2M1 = np.array([0.0, 0.5, 1.0, 1.5, 2.0, 3.0, 4.0, 6.0, -0.0, -0.5, -1.0, -1.5, -2.0, -3.0, -4.0, -6.0])


def pack_weight(w, fmt):
    k, n = w.shape
    w = f64(bf(w)).reshape(k // 32, 32, n)
    amax = np.abs(w).max(1)
    if fmt == "e4m3":
        byte = np.frexp(amax)[1] - 1 + 127 - 7
    else:
        mant, ex = np.frexp(amax / 6.0)
        byte = np.where(mant > 0.5, ex, ex - 1) + 127
    byte = np.clip(np.where(amax > 0, byte, 1), 1, 254)
    scaled = (w * np.exp2(127.0 - byte)[:, None, :]).reshape(k, n).astype(np.float32)
    by_word = np.ascontiguousarray(scaled.reshape(k // 512, 128, 4, n).transpose(0, 1, 3, 2))
    if fmt == "e4m3":
        words = by_word.astype(ml_dtypes.float8_e4m3fn).view(np.uint8)
    else:
        c = by_word.astype(ml_dtypes.float4_e2m1fn).view(np.uint8) & 0xF
        words = c[..., 0::2] | (c[..., 1::2] << 4)
    return np.ascontiguousarray(words), np.ascontiguousarray(byte.astype(np.uint8).reshape(k // 512, 16, n))


def unpack_weight(words, scales, fmt):
    g, p, n, _ = words.shape
    if fmt == "e4m3":
        vals = np.ascontiguousarray(words).view(ml_dtypes.float8_e4m3fn).astype(np.float64)
    else:
        nib = np.empty((g, p, n, 4), np.uint8)
        nib[..., 0::2] = words & 0xF
        nib[..., 1::2] = words >> 4
        vals = E2M1[nib]
    vals = vals * np.repeat(np.exp2(scales.astype(np.float64) - 127.0), 8, axis=1)[..., None]
    return vals.transpose(0, 1, 3, 2).reshape(g * 512, n)
def pack4(w):
    words, scales = pack_weight(w, "e2m1")
    return words.reshape(words.shape[0], 128, -1), scales


def unpack4(words, scales):
    return unpack_weight(words.reshape(words.shape[0], 128, -1, 2), scales, "e2m1")


def planes(Y):
    n, m = Y.shape
    b = f64(bf(Y)).reshape(n // 32, 32, m)
    amax = np.abs(b).max(1)
    byte = np.clip(np.where(amax > 0, np.frexp(amax)[1] - 1 + 127 - 7, 1), 1, 254)
    codes = (b * np.exp2(127.0 - byte)[:, None, :]).reshape(n, m).astype(np.float32).astype(ml_dtypes.float8_e4m3fn).view(np.uint8)
    words = codes.reshape(n // 512, 128, 4, m).transpose(0, 1, 3, 2)
    return np.ascontiguousarray(words), np.ascontiguousarray(byte.astype(np.uint8).reshape(n // 512, 16, m))


M, P, S = 1280, 1024, 1536


def setup_inputs():
    s = mx_kscale(P)
    t = mx_kscale(S)
    size = np.exp(0.8 * np.random.randn(S))
    x = np.random.randn(P, M) * s[:, None]
    gain = np.random.randn(P, S) / np.sqrt(P) * t[None, :] / s[:, None]
    x_words, x_scales = pack_weight(f64(bf(x)), "e4m3")
    gain_words, gain_scales = pack4(f64(bf(gain)))
    forecasts = bf(np.random.randn(M, S) * t[None, :])
    transition = bf(np.random.randn(S, S) / np.sqrt(S) * size[None, :] / t[:, None])
    bias = bf(0.4 * np.random.randn(S) * size)
    return {"x_words": x_words, "x_scales": x_scales,
            "gain_words": gain_words, "gain_scales": gain_scales,
            "forecasts": forecasts, "transition": transition, "bias": bias}

def reference(x_words, x_scales, gain_words, gain_scales, forecasts, transition, bias):
    X = unpack_weight(x_words, x_scales, "e4m3")
    G = unpack4(gain_words, gain_scales)
    a = (X.T @ G) + f64(forecasts)
    y = (mxq(a, 1, "e4m3") @ mxq(f64(transition), 0, "e4m3")) + f64(bias)
    Y = y.T
    words, scales = planes(Y)
    return y, words, scales

@@ -1,0 +1,280 @@
+from contextlib import ExitStack
+
+import concourse.mybir as mybir
+from concourse.masks import make_identity
+
+M, P_OBS, S = 1280, 1024, 1536
+FLOPS = 2 * M * S * (P_OBS + S)
+
+F32 = mybir.dt.float32
+BF16 = mybir.dt.bfloat16
+I32 = mybir.dt.int32
+U32 = mybir.dt.uint32
+U8 = mybir.dt.uint8
+FP8X4 = mybir.dt.float8_e4m3fn_x4
+FP4X4 = mybir.dt.float4_e2m1fn_x4
+ADD = mybir.AluOpType.add
+
+P = 128
+W = 512
+GROUPS = S // W
+OBS_GROUPS = P_OBS // W
+TILES = M // P
+UNITS = TILES * GROUPS
+PAIRS = UNITS
+STEPS = PAIRS // 2
+ACC_BANKS = 6
+T_BANKS = 2
+X_CUTS = (0, 256, 640, 1280)
+
+
+def tile_fixed_gain_state_forecast_h2_kernel(
+    tc, x_words, x_scales, gain_words, gain_scales, forecasts, transition, bias, out_0, out_1, out_2
+):
+    nc = tc.nc
+    with ExitStack() as ctx:
+        keep = ctx.enter_context(tc.tile_pool(name="keep", bufs=1))
+        ring = ctx.enter_context(tc.tile_pool(name="ring", bufs=1))
+        psum = ctx.enter_context(tc.psum_pool(name="psum", bufs=1))
+        ctx.enter_context(tc.manual_schedule())
+
+        x_plane = keep.tile([P, OBS_GROUPS, M], U8, name="x_plane", align_bytes=64)
+        g_plane = keep.tile([P, OBS_GROUPS, S], U8, name="g_plane", align_bytes=64)
+        nc.vector.memset(x_plane[:].bitcast(I32), 0)
+        nc.gpsimd.memset(g_plane[:].bitcast(I32), 0)
+
+        x_rows = x_words.rearrange("g p m t -> p g (m t)")
+        g_rows = gain_words.rearrange("g p b -> p g b")
+        x_codes, g_codes, f_rows, a_raw = {}, {}, {}, {}
+
+        def load_x(i):
+            lo, hi = X_CUTS[i], X_CUTS[i + 1]
+            t = keep.tile([P, OBS_GROUPS, hi - lo], U32, name="x_codes%d" % i, align_bytes=64)
+            nc.sync.dma_start(out=t[:].bitcast(I32), in_=x_rows[:, :, 4 * lo : 4 * hi].bitcast(I32))
+            for mt in range(lo // P, hi // P):
+                x_codes[mt] = t[:, :, mt * P - lo : (mt + 1) * P - lo]
+
+        def load_g(n0, n1):
+            t = keep.tile([P, OBS_GROUPS, 2 * W * (n1 - n0)], U8, name="g_codes%d" % n0, align_bytes=64)
+            nc.sync.dma_start(out=t[:].bitcast(I32), in_=g_rows[:, :, 2 * W * n0 : 2 * W * n1].bitcast(I32))
+            for n in range(n0, n1):
+                g_codes[n] = t[:, :, 2 * W * (n - n0) : 2 * W * (n - n0 + 1)]
+
+        def load_scale_rows(queue, plane, scales, q):
+            queue.dma_start(
+                out=plane[32 * q : 32 * q + 4, :, :].bitcast(I32),
+                in_=scales[:, 4 * q : 4 * q + 4, :].rearrange("g r n -> r g n").bitcast(I32),
+            )
+
+        def load_f(mt):
+            t = keep.tile([P, S], BF16, name="f_rows%d" % mt, align_bytes=64)
+            nc.sync.dma_start(out=t[:], in_=forecasts[mt * P : (mt + 1) * P, :])
+            f_rows[mt] = t
+
+        def load_a(i):
+            n, g = divmod(i, GROUPS)
+            t = keep.tile([P, 4, W], BF16, name="a_raw%d" % i, align_bytes=64)
+            src = transition[g * W : (g + 1) * W, n * W : (n + 1) * W]
+            nc.sync.dma_start(out=t[:], in_=src.rearrange("(p j) w -> p j w", j=4))
+            a_raw[i] = t
+
+        load_x(0)
+        load_g(0, 1)
+        for q in range(4):
+            load_scale_rows(nc.sync, x_plane, x_scales, q)
+        for q in range(4):
+            load_scale_rows(nc.sync, g_plane, gain_scales, q)
+        ident = keep.tile([P, P], F32, name="ident", align_bytes=64)
+        make_identity(nc, ident[:])
+
+        load_g(1, 3)
+        load_f(0)
+        load_a(0)
+        load_f(1)
+        load_x(1)
+        load_a(1)
+        load_f(2)
+        load_f(3)
+        load_x(2)
+        load_a(2)
+        load_f(4)
+        for i in range(3, 8):
+            load_f(i + 2)
+            load_a(i)
+        bias_rows = keep.tile([P, S], BF16, name="bias_rows", align_bytes=64)
+        nc.sync.dma_start(out=bias_rows[:], in_=bias.partition_broadcast(P))
+        load_a(8)
+
+        tr_codes = [keep.tile([P, W], U32, name="tr_codes%d" % i, align_bytes=64) for i in range(GROUPS * GROUPS)]
+        tr_plane = [keep.tile([P, W], U8, name="tr_plane%d" % i, align_bytes=64) for i in range(GROUPS * GROUPS)]
+        st_codes = [keep.tile([P, 2 * P], U32, name="st_codes%d" % i, align_bytes=64) for i in range(UNITS // 2)]
+        st_plane = [keep.tile([P, 2 * P], U8, name="st_plane%d" % i, align_bytes=64) for i in range(UNITS // 2)]
+        y_codes = [keep.tile([P, M], U32, name="y_codes%d" % n, align_bytes=64) for n in range(GROUPS)]
+        y_plane = [keep.tile([P, M], U8, name="y_plane%d" % n, align_bytes=64) for n in range(GROUPS)]
+
+        a_grouped, acc, rounded, y_pair, bank, grouped = {}, {}, {}, {}, {}, {}
+
+        def interleave_a(i, on_vector):
+            t = keep.tile([P, W, 4], BF16, name="a_grouped%d" % i, align_bytes=64)
+            dst = t[:].rearrange("p (c i) j -> p c j i", i=4)
+            src = a_raw[i][:].rearrange("p j (c i) -> p c j i", i=4)
+            if on_vector:
+                nc.vector.tensor_copy(out=dst, in_=src)
+            else:
+                nc.scalar.copy(out=dst, in_=src)
+            a_grouped[i] = t
+
+        def quantize_a(i):
+            nc.vector.quantize_mx(
+                out=tr_codes[i][:].bitcast(FP8X4),
+                scales=tr_plane[i][:],
+                in_=a_grouped[i][:].rearrange("p w j -> p (w j)"),
+            )
+
+        def place(u):
+            if u < UNITS:
+                return divmod(u, GROUPS)
+            n, mt = divmod(u - UNITS, TILES)
+            return mt, n
+
+        def multiply(u):
+            mt, n = place(u)
+            acc[u] = psum.tile([P, W], F32, name="acc", tag="acc%d" % (u % ACC_BANKS))
+            if u < UNITS:
+                for g in range(OBS_GROUPS):
+                    nc.tensor.matmul_mx(
+                        out=acc[u][:],
+                        lhsT=x_codes[mt][:, g, :].bitcast(FP8X4),
+                        lhsT_scale=x_plane[:, g, mt * P : (mt + 1) * P],
+                        rhs=g_codes[n][:, g, :].bitcast(FP4X4),
+                        rhs_scale=g_plane[:, g, n * W : (n + 1) * W],
+                        start=(g == 0),
+                        stop=(g == OBS_GROUPS - 1),
+                    )
+            else:
+                for g in range(GROUPS):
+                    pair, j = divmod(mt * GROUPS + g, 2)
+                    nc.tensor.matmul_mx(
+                        out=acc[u][:],
+                        lhsT=st_codes[pair][:, j * P : (j + 1) * P].bitcast(FP8X4),
+                        lhsT_scale=st_plane[pair][:, j * P : (j + 1) * P],
+                        rhs=tr_codes[n * GROUPS + g][:].bitcast(FP8X4),
+                        rhs_scale=tr_plane[n * GROUPS + g][:],
+                        start=(g == 0),
+                        stop=(g == GROUPS - 1),
+                    )
+
+        def by_half(ap):
+            return ap.rearrange("p (q h e) -> p h q e", h=2, e=2)
+
+        def new_rounded(u):
+            rounded[u] = ring.tile([P, W], BF16, name="rounded", tag="rounded%d" % (u % 8), align_bytes=64)
+            return rounded[u][:].rearrange("p (h q e) -> p h q e", h=2, e=2)
+
+        def add(u):
+            mt, n = place(u)
+            cols = slice(n * W, (n + 1) * W)
+            if u < UNITS:
+                nc.vector.tensor_tensor(
+                    out=new_rounded(u), in0=by_half(acc[u][:]), in1=by_half(f_rows[mt][:, cols]), op=ADD
+                )
+            else:
+                y_pair[u] = ring.tile([P, W], F32, name="y_tile", tag="y_tile%d" % (u % 8), align_bytes=64)
+                nc.vector.tensor_tensor(out=y_pair[u][:], in0=acc[u][:], in1=bias_rows[:, cols], op=ADD)
+                nc.sync.dma_start(out=out_0[mt * P : (mt + 1) * P, cols], in_=y_pair[u][:])
+
+        def round_y(u):
+            if u >= UNITS:
+                nc.scalar.copy(out=new_rounded(u), in_=by_half(y_pair[u][:]))
+
+        def turn(pair):
+            bank[pair] = psum.tile([P, 2, 2, P], F32, name="turned", tag="turned%d" % (pair % T_BANKS))
+            for j in range(2):
+                words = rounded[2 * pair + j][:].bitcast(F32)
+                for h in range(2):
+                    nc.tensor.transpose(bank[pair][:, j, h, :], words[:, h * P : (h + 1) * P], ident[:])
+
+        def gather(pair):
+            grouped[pair] = ring.tile([P, 2 * W], BF16, name="grouped", tag="grouped%d" % (pair % 4), align_bytes=64)
+            nc.scalar.copy(
+                out=grouped[pair][:].bitcast(F32).rearrange("p (j m h) -> p j m h", j=2, h=2),
+                in_=bank[pair][:].rearrange("p j h m -> p j m h"),
+            )
+
+        def quantize(pair):
+            if 2 * pair < UNITS:
+                nc.vector.quantize_mx(
+                    out=st_codes[pair][:].bitcast(FP8X4), scales=st_plane[pair][:], in_=grouped[pair][:]
+                )
+                return
+            mt, n = place(2 * pair)
+            cols = slice(mt * P, (mt + 2) * P)
+            nc.vector.quantize_mx(
+                out=y_codes[n][:, cols].bitcast(FP8X4), scales=y_plane[n][:, cols], in_=grouped[pair][:]
+            )
+            words = out_1[n].rearrange("p m t -> p (m t)")
+            nc.sync.dma_start(
+                out=words[:, 4 * mt * P : 4 * (mt + 2) * P].bitcast(I32), in_=y_codes[n][:, cols].bitcast(I32)
+            )
+            if mt + 2 == TILES:
+                for q in range(4):
+                    queue = nc.scalar if (n == GROUPS - 1 and q % 2) else nc.sync
+                    queue.dma_start(
+                        out=out_2[n, 4 * q : 4 * q + 4, :].bitcast(I32),
+                        in_=y_plane[n][32 * q : 32 * q + 4, :].bitcast(I32),
+                    )
+
+        scalar_interleave = {1: 1, 2: 2, 3: 3, 4: 4, 5: 5, 6: 6}
+        vector_interleave = {8: 7, 10: 8}
+        quantize_step = {1: 0, 3: 1, 5: 2, 7: 3, 8: 4, 9: 5, 10: 6, 11: 7, 12: 8}
+
+        interleave_a(0, True)
+        for step in range(STEPS - 1):
+            units = range(4 * step, 4 * step + 4)
+            late = [2 * (step - 2), 2 * (step - 2) + 1] if step >= 2 else []
+            mid = [2 * (step - 1), 2 * (step - 1) + 1] if step >= 1 else []
+            if step in scalar_interleave:
+                interleave_a(scalar_interleave[step], False)
+            if step in quantize_step:
+                quantize_a(quantize_step[step])
+            for i in range(4):
+                multiply(units[i])
+                add(units[i])
+                if i < 3:
+                    round_y(units[i])
+                if late and i in (0, 2):
+                    quantize(late[i // 2])
+                if i == 1 and step in vector_interleave:
+                    interleave_a(vector_interleave[step], True)
+            for pair in mid:
+                turn(pair)
+            if mid:
+                gather(mid[0])
+            round_y(units[3])
+            if mid:
+                gather(mid[1])
+
+        last = PAIRS - 1
+        for j in range(2):
+            multiply(2 * last - 2 + j)
+            add(2 * last - 2 + j)
+            round_y(2 * last - 2 + j)
+            quantize(last - 5 + j)
+        for pair in (last - 3, last - 2):
+            turn(pair)
+            gather(pair)
+        multiply(2 * last)
+        add(2 * last)
+        round_y(2 * last)
+        quantize(last - 3)
+        u = 2 * last + 1
+        multiply(u)
+        nc.vector.tensor_tensor(
+            out=new_rounded(u), in0=by_half(acc[u][:]), in1=by_half(bias_rows[:, S - W :]), op=ADD
+        )
+        add(u)
+        quantize(last - 2)
+        for pair in (last - 1, last):
+            turn(pair)
+            gather(pair)
+            quantize(pair)

@@ -14,6 +14,7 @@ U8 = mybir.dt.uint8
 FP8X4 = mybir.dt.float8_e4m3fn_x4
 FP4X4 = mybir.dt.float4_e2m1fn_x4
 ADD = mybir.AluOpType.add
+MULT = mybir.AluOpType.mult
 
 P = 128
 W = 512
@@ -90,20 +91,27 @@ def tile_fixed_gain_state_forecast_h2_kernel(
         load_g(1, 3)
         load_f(0)
         load_a(0)
+        bias_cols = keep.tile([P, GROUPS, 4], BF16, name="bias_cols", align_bytes=64)
+        nc.sync.dma_start(out=bias_cols[:], in_=bias.rearrange("(n p j) -> p n j", p=P, j=4))
         load_f(1)
         load_x(1)
         load_a(1)
         load_f(2)
         load_f(3)
-        load_x(2)
         load_a(2)
         load_f(4)
-        for i in range(3, 8):
-            load_f(i + 2)
+        load_x(2)
+        load_a(3)
+        load_f(5)
+        load_f(6)
+        load_a(4)
+        load_f(7)
+        load_f(8)
+        load_a(5)
+        load_f(9)
+        for i in range(6, 9):
             load_a(i)
         bias_rows = keep.tile([P, S], BF16, name="bias_rows", align_bytes=64)
-        nc.sync.dma_start(out=bias_rows[:], in_=bias.partition_broadcast(P))
-        load_a(8)
 
         tr_codes = [keep.tile([P, W], U32, name="tr_codes%d" % i, align_bytes=64) for i in range(GROUPS * GROUPS)]
         tr_plane = [keep.tile([P, W], U8, name="tr_plane%d" % i, align_bytes=64) for i in range(GROUPS * GROUPS)]
@@ -114,15 +122,28 @@ def tile_fixed_gain_state_forecast_h2_kernel(
 
         a_grouped, acc, rounded, y_pair, bank, grouped = {}, {}, {}, {}, {}, {}
 
-        def interleave_a(i, on_vector):
-            t = keep.tile([P, W, 4], BF16, name="a_grouped%d" % i, align_bytes=64)
-            dst = t[:].rearrange("p (c i) j -> p c j i", i=4)
-            src = a_raw[i][:].rearrange("p j (c i) -> p c j i", i=4)
-            if on_vector:
-                nc.vector.tensor_copy(out=dst, in_=src)
-            else:
-                nc.scalar.copy(out=dst, in_=src)
-            a_grouped[i] = t
+        def interleave_a(i, half, engine_copy):
+            if half == 0:
+                a_grouped[i] = keep.tile([P, W, 4], BF16, name="a_grouped%d" % i, align_bytes=64)
+            cols = slice(half * W // 2, (half + 1) * W // 2)
+            engine_copy(
+                out=a_grouped[i][:, cols, :].rearrange("p (c i) j -> p c j i", i=4),
+                in_=a_raw[i][:, :, cols].rearrange("p j (c i) -> p c j i", i=4),
+            )
+
+        def spread_bias():
+            for first, count in ((0, 2), (2, 1)):
+                spread = psum.tile([P, 2, 2, P], F32, name="turned", tag="turned%d" % (first // 2))
+                for j in range(count):
+                    words = bias_cols[:, first + j, :].bitcast(F32)
+                    for h in range(2):
+                        nc.tensor.transpose(spread[:, j, h, :], words[:, h : h + 1].to_broadcast([P, P]), ident[:])
+                nc.scalar.copy(
+                    out=bias_rows[:, first * W : (first + count) * W]
+                    .bitcast(F32)
+                    .rearrange("p (j m h) -> p j m h", j=count, h=2),
+                    in_=spread[:, :count].rearrange("p j h m -> p j m h"),
+                )
 
         def quantize_a(i):
             nc.vector.quantize_mx(
@@ -184,7 +205,13 @@ def tile_fixed_gain_state_forecast_h2_kernel(
                 nc.sync.dma_start(out=out_0[mt * P : (mt + 1) * P, cols], in_=y_pair[u][:])
 
         def round_y(u):
-            if u >= UNITS:
+            if u < UNITS:
+                return
+            if u % 4 < 2:
+                nc.gpsimd.tensor_scalar(
+                    out=new_rounded(u), in0=by_half(y_pair[u][:]), scalar1=1.0, scalar2=0.0, op0=MULT, op1=ADD
+                )
+            else:
                 nc.scalar.copy(out=new_rounded(u), in_=by_half(y_pair[u][:]))
 
         def turn(pair):
@@ -224,17 +251,15 @@ def tile_fixed_gain_state_forecast_h2_kernel(
                         in_=y_plane[n][32 * q : 32 * q + 4, :].bitcast(I32),
                     )
 
-        scalar_interleave = {1: 1, 2: 2, 3: 3, 4: 4, 5: 5, 6: 6}
-        vector_interleave = {8: 7, 10: 8}
         quantize_step = {1: 0, 3: 1, 5: 2, 7: 3, 8: 4, 9: 5, 10: 6, 11: 7, 12: 8}
 
-        interleave_a(0, True)
         for step in range(STEPS - 1):
             units = range(4 * step, 4 * step + 4)
             late = [2 * (step - 2), 2 * (step - 2) + 1] if step >= 2 else []
             mid = [2 * (step - 1), 2 * (step - 1) + 1] if step >= 1 else []
-            if step in scalar_interleave:
-                interleave_a(scalar_interleave[step], False)
+            for h in range(18):
+                if step == 2 * h // 3:
+                    interleave_a(h // 2, h % 2, nc.scalar.copy)
             if step in quantize_step:
                 quantize_a(quantize_step[step])
             for i in range(4):
@@ -244,8 +269,8 @@ def tile_fixed_gain_state_forecast_h2_kernel(
                     round_y(units[i])
                 if late and i in (0, 2):
                     quantize(late[i // 2])
-                if i == 1 and step in vector_interleave:
-                    interleave_a(vector_interleave[step], True)
+            if step == 0:
+                spread_bias()
             for pair in mid:
                 turn(pair)
             if mid:

@@ -21,12 +21,24 @@ W = 512
 GROUPS = S // W
 OBS_GROUPS = P_OBS // W
 TILES = M // P
-UNITS = TILES * GROUPS
-PAIRS = UNITS
-STEPS = PAIRS // 2
-ACC_BANKS = 6
-T_BANKS = 2
-X_CUTS = (0, 256, 640, 1280)
+STAGE_UNITS = TILES * GROUPS
+LAST_UNIT = 2 * STAGE_UNITS - 1
+LAST_PAIR = STAGE_UNITS - 1
+PIECES = GROUPS * GROUPS
+
+STEP_PAIRS = 3
+STEP_UNITS = 2 * STEP_PAIRS
+STEPS = 2 * STAGE_UNITS // STEP_UNITS
+STEP_TILES = STEP_UNITS // GROUPS
+ACC_BANKS = 8 - STEP_PAIRS
+LEAD = 4
+GPSIMD_UNITS = (0, 2)
+HALVES, HALF_STEPS = 7, 3
+WORD_CUTS = (0, 4, 8, 10)
+ROUNDED_BUFS = 2 * STEP_UNITS
+TURNED_BUFS = 2 * STEP_PAIRS
+Y_BUFS = 8
+PIECE_BUFS = 5
 
 
 def tile_fixed_gain_state_forecast_h2_kernel(
@@ -46,14 +58,15 @@ def tile_fixed_gain_state_forecast_h2_kernel(
 
         x_rows = x_words.rearrange("g p m t -> p g (m t)")
         g_rows = gain_words.rearrange("g p b -> p g b")
-        x_codes, g_codes, f_rows, a_raw = {}, {}, {}, {}
+        x_codes, g_codes, f_rows, a_rows = {}, {}, {}, {}
 
-        def load_x(i):
-            lo, hi = X_CUTS[i], X_CUTS[i + 1]
-            t = keep.tile([P, OBS_GROUPS, hi - lo], U32, name="x_codes%d" % i, align_bytes=64)
-            nc.sync.dma_start(out=t[:].bitcast(I32), in_=x_rows[:, :, 4 * lo : 4 * hi].bitcast(I32))
-            for mt in range(lo // P, hi // P):
-                x_codes[mt] = t[:, :, mt * P - lo : (mt + 1) * P - lo]
+        def load_x(step):
+            width = STEP_TILES * P
+            t = keep.tile([P, OBS_GROUPS, width], U32, name="x_codes%d" % step, align_bytes=64)
+            src = x_rows[:, :, 4 * width * step : 4 * width * (step + 1)]
+            nc.sync.dma_start(out=t[:].bitcast(I32), in_=src.bitcast(I32))
+            for j in range(STEP_TILES):
+                x_codes[STEP_TILES * step + j] = t[:, :, j * P : (j + 1) * P]
 
         def load_g(n0, n1):
             t = keep.tile([P, OBS_GROUPS, 2 * W * (n1 - n0)], U8, name="g_codes%d" % n0, align_bytes=64)
@@ -61,107 +74,94 @@ def tile_fixed_gain_state_forecast_h2_kernel(
             for n in range(n0, n1):
                 g_codes[n] = t[:, :, 2 * W * (n - n0) : 2 * W * (n - n0 + 1)]
 
-        def load_scale_rows(queue, plane, scales, q):
-            queue.dma_start(
-                out=plane[32 * q : 32 * q + 4, :, :].bitcast(I32),
-                in_=scales[:, 4 * q : 4 * q + 4, :].rearrange("g r n -> r g n").bitcast(I32),
-            )
+        def load_plane(plane, scales):
+            for quad in range(4):
+                nc.sync.dma_start(
+                    out=plane[32 * quad : 32 * quad + 4, :, :].bitcast(I32),
+                    in_=scales[:, 4 * quad : 4 * quad + 4, :].rearrange("g r n -> r g n").bitcast(I32),
+                )
 
         def load_f(mt):
-            t = keep.tile([P, S], BF16, name="f_rows%d" % mt, align_bytes=64)
-            nc.sync.dma_start(out=t[:], in_=forecasts[mt * P : (mt + 1) * P, :])
-            f_rows[mt] = t
+            f_rows[mt] = keep.tile([P, S], BF16, name="f_rows%d" % mt, align_bytes=64)
+            nc.sync.dma_start(out=f_rows[mt][:], in_=forecasts[mt * P : (mt + 1) * P, :])
 
-        def load_a(i):
-            n, g = divmod(i, GROUPS)
-            t = keep.tile([P, 4, W], BF16, name="a_raw%d" % i, align_bytes=64)
+        def load_a(piece):
+            n, g = divmod(piece, GROUPS)
+            a_rows[piece] = keep.tile([P, 4, W], BF16, name="a_rows%d" % piece, align_bytes=64)
             src = transition[g * W : (g + 1) * W, n * W : (n + 1) * W]
-            nc.sync.dma_start(out=t[:], in_=src.rearrange("(p j) w -> p j w", j=4))
-            a_raw[i] = t
+            nc.sync.dma_start(out=a_rows[piece][:], in_=src.rearrange("(p t) w -> p t w", t=4))
 
         load_x(0)
         load_g(0, 1)
-        for q in range(4):
-            load_scale_rows(nc.sync, x_plane, x_scales, q)
-        for q in range(4):
-            load_scale_rows(nc.sync, g_plane, gain_scales, q)
+        load_plane(x_plane, x_scales)
+        load_plane(g_plane, gain_scales)
         ident = keep.tile([P, P], F32, name="ident", align_bytes=64)
         make_identity(nc, ident[:])
-
-        load_g(1, 3)
+        load_g(1, GROUPS)
         load_f(0)
         load_a(0)
         bias_cols = keep.tile([P, GROUPS, 4], BF16, name="bias_cols", align_bytes=64)
-        nc.sync.dma_start(out=bias_cols[:], in_=bias.rearrange("(n p j) -> p n j", p=P, j=4))
+        nc.sync.dma_start(out=bias_cols[:], in_=bias.rearrange("(n p t) -> p n t", p=P, t=4))
         load_f(1)
-        load_x(1)
-        load_a(1)
-        load_f(2)
-        load_f(3)
-        load_a(2)
-        load_f(4)
-        load_x(2)
-        load_a(3)
-        load_f(5)
-        load_f(6)
-        load_a(4)
-        load_f(7)
-        load_f(8)
-        load_a(5)
-        load_f(9)
-        for i in range(6, 9):
-            load_a(i)
-        bias_rows = keep.tile([P, S], BF16, name="bias_rows", align_bytes=64)
+        for step in range(1, TILES // STEP_TILES):
+            load_x(step)
+            load_a(step)
+            for j in range(STEP_TILES):
+                load_f(STEP_TILES * step + j)
+        for piece in range(TILES // STEP_TILES, PIECES):
+            load_a(piece)
 
-        tr_codes = [keep.tile([P, W], U32, name="tr_codes%d" % i, align_bytes=64) for i in range(GROUPS * GROUPS)]
-        tr_plane = [keep.tile([P, W], U8, name="tr_plane%d" % i, align_bytes=64) for i in range(GROUPS * GROUPS)]
-        st_codes = [keep.tile([P, 2 * P], U32, name="st_codes%d" % i, align_bytes=64) for i in range(UNITS // 2)]
-        st_plane = [keep.tile([P, 2 * P], U8, name="st_plane%d" % i, align_bytes=64) for i in range(UNITS // 2)]
+        bias_rows = keep.tile([P, S], BF16, name="bias_rows", align_bytes=64)
+        tr_codes = [keep.tile([P, W], U32, name="tr_codes%d" % i, align_bytes=64) for i in range(PIECES)]
+        tr_plane = [keep.tile([P, W], U8, name="tr_plane%d" % i, align_bytes=64) for i in range(PIECES)]
+        st_codes = [keep.tile([P, 2 * P], U32, name="st_codes%d" % i, align_bytes=64) for i in range(STAGE_UNITS // 2)]
+        st_plane = [keep.tile([P, 2 * P], U8, name="st_plane%d" % i, align_bytes=64) for i in range(STAGE_UNITS // 2)]
         y_codes = [keep.tile([P, M], U32, name="y_codes%d" % n, align_bytes=64) for n in range(GROUPS)]
         y_plane = [keep.tile([P, M], U8, name="y_plane%d" % n, align_bytes=64) for n in range(GROUPS)]
+        a_grouped, acc, rounded, y_tile, turned = {}, {}, {}, {}, {}
 
-        a_grouped, acc, rounded, y_pair, bank, grouped = {}, {}, {}, {}, {}, {}
+        def lay_out_a(half):
+            piece = half // 2
+            if half % 2 == 0:
+                tag = "a_grouped%d" % (piece % PIECE_BUFS)
+                a_grouped[piece] = ring.tile([P, W, 4], BF16, name="a_grouped", tag=tag, align_bytes=64)
+            cols = slice(half % 2 * W // 2, (half % 2 + 1) * W // 2)
+            nc.scalar.copy(
+                out=a_grouped[piece][:, cols, :].rearrange("p (c i) t -> p c t i", i=4),
+                in_=a_rows[piece][:, :, cols].rearrange("p t (c i) -> p c t i", i=4),
+            )
 
-        def interleave_a(i, half, engine_copy):
-            if half == 0:
-                a_grouped[i] = keep.tile([P, W, 4], BF16, name="a_grouped%d" % i, align_bytes=64)
-            cols = slice(half * W // 2, (half + 1) * W // 2)
-            engine_copy(
-                out=a_grouped[i][:, cols, :].rearrange("p (c i) j -> p c j i", i=4),
-                in_=a_raw[i][:, :, cols].rearrange("p j (c i) -> p c j i", i=4),
+        def quantize_a(piece):
+            nc.vector.quantize_mx(
+                out=tr_codes[piece][:].bitcast(FP8X4),
+                scales=tr_plane[piece][:],
+                in_=a_grouped[piece][:].rearrange("p w t -> p (w t)"),
             )
 
         def spread_bias():
-            for first, count in ((0, 2), (2, 1)):
-                spread = psum.tile([P, 2, 2, P], F32, name="turned", tag="turned%d" % (first // 2))
+            for bank_no, n0 in enumerate(range(0, GROUPS, 2)):
+                count = min(2, GROUPS - n0)
+                bank = psum.tile([P, 2, 2, P], F32, name="bank", tag="bank%d" % bank_no)
                 for j in range(count):
-                    words = bias_cols[:, first + j, :].bitcast(F32)
+                    words = bias_cols[:, n0 + j, :].bitcast(F32)
                     for h in range(2):
-                        nc.tensor.transpose(spread[:, j, h, :], words[:, h : h + 1].to_broadcast([P, P]), ident[:])
+                        nc.tensor.transpose(bank[:, j, h, :], words[:, h : h + 1].to_broadcast([P, P]), ident[:])
+                dst = bias_rows[:, n0 * W : (n0 + count) * W].bitcast(F32)
                 nc.scalar.copy(
-                    out=bias_rows[:, first * W : (first + count) * W]
-                    .bitcast(F32)
-                    .rearrange("p (j m h) -> p j m h", j=count, h=2),
-                    in_=spread[:, :count].rearrange("p j h m -> p j m h"),
+                    out=dst.rearrange("p (j q h) -> p j q h", j=count, h=2),
+                    in_=bank[:, :count].rearrange("p j h q -> p j q h"),
                 )
 
-        def quantize_a(i):
-            nc.vector.quantize_mx(
-                out=tr_codes[i][:].bitcast(FP8X4),
-                scales=tr_plane[i][:],
-                in_=a_grouped[i][:].rearrange("p w j -> p (w j)"),
-            )
-
         def place(u):
-            if u < UNITS:
+            if u < STAGE_UNITS:
                 return divmod(u, GROUPS)
-            n, mt = divmod(u - UNITS, TILES)
+            n, mt = divmod(u - STAGE_UNITS, TILES)
             return mt, n
 
         def multiply(u):
             mt, n = place(u)
             acc[u] = psum.tile([P, W], F32, name="acc", tag="acc%d" % (u % ACC_BANKS))
-            if u < UNITS:
+            if u < STAGE_UNITS:
                 for g in range(OBS_GROUPS):
                     nc.tensor.matmul_mx(
                         out=acc[u][:],
@@ -189,117 +189,108 @@ def tile_fixed_gain_state_forecast_h2_kernel(
             return ap.rearrange("p (q h e) -> p h q e", h=2, e=2)
 
         def new_rounded(u):
-            rounded[u] = ring.tile([P, W], BF16, name="rounded", tag="rounded%d" % (u % 8), align_bytes=64)
+            tag = "rounded%d" % (u % ROUNDED_BUFS)
+            rounded[u] = ring.tile([P, W], BF16, name="rounded", tag=tag, align_bytes=64)
             return rounded[u][:].rearrange("p (h q e) -> p h q e", h=2, e=2)
+
+        def add_rounded(u, addend):
+            nc.vector.tensor_tensor(out=new_rounded(u), in0=by_half(acc[u][:]), in1=by_half(addend), op=ADD)
 
         def add(u):
             mt, n = place(u)
             cols = slice(n * W, (n + 1) * W)
-            if u < UNITS:
-                nc.vector.tensor_tensor(
-                    out=new_rounded(u), in0=by_half(acc[u][:]), in1=by_half(f_rows[mt][:, cols]), op=ADD
-                )
-            else:
-                y_pair[u] = ring.tile([P, W], F32, name="y_tile", tag="y_tile%d" % (u % 8), align_bytes=64)
-                nc.vector.tensor_tensor(out=y_pair[u][:], in0=acc[u][:], in1=bias_rows[:, cols], op=ADD)
-                nc.sync.dma_start(out=out_0[mt * P : (mt + 1) * P, cols], in_=y_pair[u][:])
+            if u < STAGE_UNITS:
+                add_rounded(u, f_rows[mt][:, cols])
+                return
+            if u == LAST_UNIT:
+                add_rounded(u, bias_rows[:, cols])
+            y_tile[u] = ring.tile([P, W], F32, name="y_tile", tag="y_tile%d" % (u % Y_BUFS), align_bytes=64)
+            nc.vector.tensor_tensor(out=y_tile[u][:], in0=acc[u][:], in1=bias_rows[:, cols], op=ADD)
+            nc.sync.dma_start(out=out_0[mt * P : (mt + 1) * P, cols], in_=y_tile[u][:])
 
         def round_y(u):
-            if u < UNITS:
+            if u < STAGE_UNITS or u == LAST_UNIT:
                 return
-            if u % 4 < 2:
+            if u % STEP_UNITS in GPSIMD_UNITS or u == LAST_UNIT - 2:
                 nc.gpsimd.tensor_scalar(
-                    out=new_rounded(u), in0=by_half(y_pair[u][:]), scalar1=1.0, scalar2=0.0, op0=MULT, op1=ADD
+                    out=new_rounded(u), in0=by_half(y_tile[u][:]), scalar1=1.0, scalar2=0.0, op0=MULT, op1=ADD
                 )
             else:
-                nc.scalar.copy(out=new_rounded(u), in_=by_half(y_pair[u][:]))
+                nc.scalar.copy(out=new_rounded(u), in_=by_half(y_tile[u][:]))
 
         def turn(pair):
-            bank[pair] = psum.tile([P, 2, 2, P], F32, name="turned", tag="turned%d" % (pair % T_BANKS))
+            bank = psum.tile([P, 2, 2, P], F32, name="bank", tag="bank%d" % (pair % STEP_PAIRS))
             for j in range(2):
                 words = rounded[2 * pair + j][:].bitcast(F32)
                 for h in range(2):
-                    nc.tensor.transpose(bank[pair][:, j, h, :], words[:, h * P : (h + 1) * P], ident[:])
-
-        def gather(pair):
-            grouped[pair] = ring.tile([P, 2 * W], BF16, name="grouped", tag="grouped%d" % (pair % 4), align_bytes=64)
+                    nc.tensor.transpose(bank[:, j, h, :], words[:, h * P : (h + 1) * P], ident[:])
+            tag = "turned%d" % (pair % TURNED_BUFS)
+            turned[pair] = ring.tile([P, 2 * W], BF16, name="turned", tag=tag, align_bytes=64)
             nc.scalar.copy(
-                out=grouped[pair][:].bitcast(F32).rearrange("p (j m h) -> p j m h", j=2, h=2),
-                in_=bank[pair][:].rearrange("p j h m -> p j m h"),
+                out=turned[pair][:].bitcast(F32).rearrange("p (j m h) -> p j m h", j=2, h=2),
+                in_=bank[:].rearrange("p j h m -> p j m h"),
             )
 
         def quantize(pair):
-            if 2 * pair < UNITS:
+            if 2 * pair < STAGE_UNITS:
                 nc.vector.quantize_mx(
-                    out=st_codes[pair][:].bitcast(FP8X4), scales=st_plane[pair][:], in_=grouped[pair][:]
+                    out=st_codes[pair][:].bitcast(FP8X4), scales=st_plane[pair][:], in_=turned[pair][:]
                 )
                 return
             mt, n = place(2 * pair)
             cols = slice(mt * P, (mt + 2) * P)
             nc.vector.quantize_mx(
-                out=y_codes[n][:, cols].bitcast(FP8X4), scales=y_plane[n][:, cols], in_=grouped[pair][:]
+                out=y_codes[n][:, cols].bitcast(FP8X4), scales=y_plane[n][:, cols], in_=turned[pair][:]
             )
-            words = out_1[n].rearrange("p m t -> p (m t)")
-            nc.sync.dma_start(
-                out=words[:, 4 * mt * P : 4 * (mt + 2) * P].bitcast(I32), in_=y_codes[n][:, cols].bitcast(I32)
-            )
+            if mt + 2 in WORD_CUTS:
+                lo, hi = P * WORD_CUTS[WORD_CUTS.index(mt + 2) - 1], P * (mt + 2)
+                dst = out_1[n].rearrange("p m t -> p (m t)")
+                nc.sync.dma_start(out=dst[:, 4 * lo : 4 * hi].bitcast(I32), in_=y_codes[n][:, lo:hi].bitcast(I32))
             if mt + 2 == TILES:
-                for q in range(4):
-                    queue = nc.scalar if (n == GROUPS - 1 and q % 2) else nc.sync
+                for quad in range(4):
+                    queue = nc.scalar if (pair == LAST_PAIR and quad % 2) else nc.sync
                     queue.dma_start(
-                        out=out_2[n, 4 * q : 4 * q + 4, :].bitcast(I32),
-                        in_=y_plane[n][32 * q : 32 * q + 4, :].bitcast(I32),
+                        out=out_2[n, 4 * quad : 4 * quad + 4, :].bitcast(I32),
+                        in_=y_plane[n][32 * quad : 32 * quad + 4, :].bitcast(I32),
                     )
 
-        quantize_step = {1: 0, 3: 1, 5: 2, 7: 3, 8: 4, 9: 5, 10: 6, 11: 7, 12: 8}
-
-        for step in range(STEPS - 1):
-            units = range(4 * step, 4 * step + 4)
-            late = [2 * (step - 2), 2 * (step - 2) + 1] if step >= 2 else []
-            mid = [2 * (step - 1), 2 * (step - 1) + 1] if step >= 1 else []
-            for h in range(18):
-                if step == 2 * h // 3:
-                    interleave_a(h // 2, h % 2, nc.scalar.copy)
-            if step in quantize_step:
-                quantize_a(quantize_step[step])
-            for i in range(4):
-                multiply(units[i])
-                add(units[i])
-                if i < 3:
-                    round_y(units[i])
-                if late and i in (0, 2):
-                    quantize(late[i // 2])
-            if step == 0:
-                spread_bias()
-            for pair in mid:
-                turn(pair)
-            if mid:
-                gather(mid[0])
-            round_y(units[3])
-            if mid:
-                gather(mid[1])
-
-        last = PAIRS - 1
-        for j in range(2):
-            multiply(2 * last - 2 + j)
-            add(2 * last - 2 + j)
-            round_y(2 * last - 2 + j)
-            quantize(last - 5 + j)
-        for pair in (last - 3, last - 2):
+        quantize_after = {}
+        for step in range(STEPS):
+            first = STEP_UNITS * step
+            last_step = step == STEPS - 1
+            halves = [half for half in range(2 * PIECES) if HALF_STEPS * half // HALVES == step]
+            pieces = [i for i in range(PIECES) if step == (i + 1 if i < PIECES - 2 else i)]
+            pairs = list(range(STEP_PAIRS * max(step - 1, 0), STEP_PAIRS * step + last_step))
+            early_halves = halves[:-1] or halves
+            for half in early_halves:
+                lay_out_a(half)
+            for i in range(STEP_UNITS):
+                u = first + i
+                if i % 2 == 0 and i // 2 < len(pieces):
+                    quantize_a(pieces[i // 2])
+                multiply(u)
+                add(u)
+                if u in quantize_after:
+                    quantize(quantize_after[u])
+                if i != LEAD - 1:
+                    round_y(u)
+                elif last_step:
+                    round_y(u)
+                    for j, pair in enumerate(pairs):
+                        turn(pair)
+                        if j < 2:
+                            quantize(pair)
+                        else:
+                            quantize_after[u + j - 1] = pair
+                else:
+                    if step == 0:
+                        spread_bias()
+                    for j, pair in enumerate(pairs):
+                        turn(pair)
+                        quantize_after[u + j + 1] = pair
+                    round_y(u)
+                    for half in halves[len(early_halves) :]:
+                        lay_out_a(half)
+        for pair in (LAST_PAIR - 1, LAST_PAIR):
             turn(pair)
-            gather(pair)
-        multiply(2 * last)
-        add(2 * last)
-        round_y(2 * last)
-        quantize(last - 3)
-        u = 2 * last + 1
-        multiply(u)
-        nc.vector.tensor_tensor(
-            out=new_rounded(u), in0=by_half(acc[u][:]), in1=by_half(bias_rows[:, S - W :]), op=ADD
-        )
-        add(u)
-        quantize(last - 2)
-        for pair in (last - 1, last):
-            turn(pair)
-            gather(pair)
             quantize(pair)

from contextlib import ExitStack

import concourse.mybir as mybir
from concourse.masks import make_identity

M, P_OBS, S = 1280, 1024, 1536
FLOPS = 2 * M * S * (P_OBS + S)

F32 = mybir.dt.float32
BF16 = mybir.dt.bfloat16
I32 = mybir.dt.int32
U32 = mybir.dt.uint32
U8 = mybir.dt.uint8
FP8X4 = mybir.dt.float8_e4m3fn_x4
FP4X4 = mybir.dt.float4_e2m1fn_x4
ADD = mybir.AluOpType.add
MULT = mybir.AluOpType.mult

P = 128
W = 512
GROUPS = S // W
OBS_GROUPS = P_OBS // W
TILES = M // P
STAGE_UNITS = TILES * GROUPS
LAST_UNIT = 2 * STAGE_UNITS - 1
LAST_PAIR = STAGE_UNITS - 1
PIECES = GROUPS * GROUPS

STEP_PAIRS = 3
STEP_UNITS = 2 * STEP_PAIRS
STEPS = 2 * STAGE_UNITS // STEP_UNITS
STEP_TILES = STEP_UNITS // GROUPS
ACC_BANKS = 8 - STEP_PAIRS
LEAD = 4
GPSIMD_UNITS = (0, 2)
HALVES, HALF_STEPS = 7, 3
WORD_CUTS = (0, 4, 8, 10)
ROUNDED_BUFS = 2 * STEP_UNITS
TURNED_BUFS = 2 * STEP_PAIRS
Y_BUFS = 8
PIECE_BUFS = 5


def tile_fixed_gain_state_forecast_h2_kernel(
    tc, x_words, x_scales, gain_words, gain_scales, forecasts, transition, bias, out_0, out_1, out_2
):
    nc = tc.nc
    with ExitStack() as ctx:
        keep = ctx.enter_context(tc.tile_pool(name="keep", bufs=1))
        ring = ctx.enter_context(tc.tile_pool(name="ring", bufs=1))
        psum = ctx.enter_context(tc.psum_pool(name="psum", bufs=1))
        ctx.enter_context(tc.manual_schedule())

        x_plane = keep.tile([P, OBS_GROUPS, M], U8, name="x_plane", align_bytes=64)
        g_plane = keep.tile([P, OBS_GROUPS, S], U8, name="g_plane", align_bytes=64)
        nc.vector.memset(x_plane[:].bitcast(I32), 0)
        nc.gpsimd.memset(g_plane[:].bitcast(I32), 0)

        x_rows = x_words.rearrange("g p m t -> p g (m t)")
        g_rows = gain_words.rearrange("g p b -> p g b")
        x_codes, g_codes, f_rows, a_rows = {}, {}, {}, {}

        def load_x(step):
            width = STEP_TILES * P
            t = keep.tile([P, OBS_GROUPS, width], U32, name="x_codes%d" % step, align_bytes=64)
            src = x_rows[:, :, 4 * width * step : 4 * width * (step + 1)]
            nc.sync.dma_start(out=t[:].bitcast(I32), in_=src.bitcast(I32))
            for j in range(STEP_TILES):
                x_codes[STEP_TILES * step + j] = t[:, :, j * P : (j + 1) * P]

        def load_g(n0, n1):
            t = keep.tile([P, OBS_GROUPS, 2 * W * (n1 - n0)], U8, name="g_codes%d" % n0, align_bytes=64)
            nc.sync.dma_start(out=t[:].bitcast(I32), in_=g_rows[:, :, 2 * W * n0 : 2 * W * n1].bitcast(I32))
            for n in range(n0, n1):
                g_codes[n] = t[:, :, 2 * W * (n - n0) : 2 * W * (n - n0 + 1)]

        def load_plane(plane, scales):
            for quad in range(4):
                nc.sync.dma_start(
                    out=plane[32 * quad : 32 * quad + 4, :, :].bitcast(I32),
                    in_=scales[:, 4 * quad : 4 * quad + 4, :].rearrange("g r n -> r g n").bitcast(I32),
                )

        def load_f(mt):
            f_rows[mt] = keep.tile([P, S], BF16, name="f_rows%d" % mt, align_bytes=64)
            nc.sync.dma_start(out=f_rows[mt][:], in_=forecasts[mt * P : (mt + 1) * P, :])

        def load_a(piece):
            n, g = divmod(piece, GROUPS)
            a_rows[piece] = keep.tile([P, 4, W], BF16, name="a_rows%d" % piece, align_bytes=64)
            src = transition[g * W : (g + 1) * W, n * W : (n + 1) * W]
            nc.sync.dma_start(out=a_rows[piece][:], in_=src.rearrange("(p t) w -> p t w", t=4))

        load_x(0)
        load_g(0, 1)
        load_plane(x_plane, x_scales)
        load_plane(g_plane, gain_scales)
        ident = keep.tile([P, P], F32, name="ident", align_bytes=64)
        make_identity(nc, ident[:])
        load_g(1, GROUPS)
        load_f(0)
        load_a(0)
        bias_cols = keep.tile([P, GROUPS, 4], BF16, name="bias_cols", align_bytes=64)
        nc.sync.dma_start(out=bias_cols[:], in_=bias.rearrange("(n p t) -> p n t", p=P, t=4))
        load_f(1)
        for step in range(1, TILES // STEP_TILES):
            load_x(step)
            load_a(step)
            for j in range(STEP_TILES):
                load_f(STEP_TILES * step + j)
        for piece in range(TILES // STEP_TILES, PIECES):
            load_a(piece)

        bias_rows = keep.tile([P, S], BF16, name="bias_rows", align_bytes=64)
        tr_codes = [keep.tile([P, W], U32, name="tr_codes%d" % i, align_bytes=64) for i in range(PIECES)]
        tr_plane = [keep.tile([P, W], U8, name="tr_plane%d" % i, align_bytes=64) for i in range(PIECES)]
        st_codes = [keep.tile([P, 2 * P], U32, name="st_codes%d" % i, align_bytes=64) for i in range(STAGE_UNITS // 2)]
        st_plane = [keep.tile([P, 2 * P], U8, name="st_plane%d" % i, align_bytes=64) for i in range(STAGE_UNITS // 2)]
        y_codes = [keep.tile([P, M], U32, name="y_codes%d" % n, align_bytes=64) for n in range(GROUPS)]
        y_plane = [keep.tile([P, M], U8, name="y_plane%d" % n, align_bytes=64) for n in range(GROUPS)]
        a_grouped, acc, rounded, y_tile, turned = {}, {}, {}, {}, {}

        def lay_out_a(half):
            piece = half // 2
            if half % 2 == 0:
                tag = "a_grouped%d" % (piece % PIECE_BUFS)
                a_grouped[piece] = ring.tile([P, W, 4], BF16, name="a_grouped", tag=tag, align_bytes=64)
            cols = slice(half % 2 * W // 2, (half % 2 + 1) * W // 2)
            nc.scalar.copy(
                out=a_grouped[piece][:, cols, :].rearrange("p (c i) t -> p c t i", i=4),
                in_=a_rows[piece][:, :, cols].rearrange("p t (c i) -> p c t i", i=4),
            )

        def quantize_a(piece):
            nc.vector.quantize_mx(
                out=tr_codes[piece][:].bitcast(FP8X4),
                scales=tr_plane[piece][:],
                in_=a_grouped[piece][:].rearrange("p w t -> p (w t)"),
            )

        def spread_bias():
            for bank_no, n0 in enumerate(range(0, GROUPS, 2)):
                count = min(2, GROUPS - n0)
                bank = psum.tile([P, 2, 2, P], F32, name="bank", tag="bank%d" % bank_no)
                for j in range(count):
                    words = bias_cols[:, n0 + j, :].bitcast(F32)
                    for h in range(2):
                        nc.tensor.transpose(bank[:, j, h, :], words[:, h : h + 1].to_broadcast([P, P]), ident[:])
                dst = bias_rows[:, n0 * W : (n0 + count) * W].bitcast(F32)
                nc.scalar.copy(
                    out=dst.rearrange("p (j q h) -> p j q h", j=count, h=2),
                    in_=bank[:, :count].rearrange("p j h q -> p j q h"),
                )

        def place(u):
            if u < STAGE_UNITS:
                return divmod(u, GROUPS)
            n, mt = divmod(u - STAGE_UNITS, TILES)
            return mt, n

        def multiply(u):
            mt, n = place(u)
            acc[u] = psum.tile([P, W], F32, name="acc", tag="acc%d" % (u % ACC_BANKS))
            if u < STAGE_UNITS:
                for g in range(OBS_GROUPS):
                    nc.tensor.matmul_mx(
                        out=acc[u][:],
                        lhsT=x_codes[mt][:, g, :].bitcast(FP8X4),
                        lhsT_scale=x_plane[:, g, mt * P : (mt + 1) * P],
                        rhs=g_codes[n][:, g, :].bitcast(FP4X4),
                        rhs_scale=g_plane[:, g, n * W : (n + 1) * W],
                        start=(g == 0),
                        stop=(g == OBS_GROUPS - 1),
                    )
            else:
                for g in range(GROUPS):
                    pair, j = divmod(mt * GROUPS + g, 2)
                    nc.tensor.matmul_mx(
                        out=acc[u][:],
                        lhsT=st_codes[pair][:, j * P : (j + 1) * P].bitcast(FP8X4),
                        lhsT_scale=st_plane[pair][:, j * P : (j + 1) * P],
                        rhs=tr_codes[n * GROUPS + g][:].bitcast(FP8X4),
                        rhs_scale=tr_plane[n * GROUPS + g][:],
                        start=(g == 0),
                        stop=(g == GROUPS - 1),
                    )

        def by_half(ap):
            return ap.rearrange("p (q h e) -> p h q e", h=2, e=2)

        def new_rounded(u):
            tag = "rounded%d" % (u % ROUNDED_BUFS)
            rounded[u] = ring.tile([P, W], BF16, name="rounded", tag=tag, align_bytes=64)
            return rounded[u][:].rearrange("p (h q e) -> p h q e", h=2, e=2)

        def add_rounded(u, addend):
            nc.vector.tensor_tensor(out=new_rounded(u), in0=by_half(acc[u][:]), in1=by_half(addend), op=ADD)

        def add(u):
            mt, n = place(u)
            cols = slice(n * W, (n + 1) * W)
            if u < STAGE_UNITS:
                add_rounded(u, f_rows[mt][:, cols])
                return
            if u == LAST_UNIT:
                add_rounded(u, bias_rows[:, cols])
            y_tile[u] = ring.tile([P, W], F32, name="y_tile", tag="y_tile%d" % (u % Y_BUFS), align_bytes=64)
            nc.vector.tensor_tensor(out=y_tile[u][:], in0=acc[u][:], in1=bias_rows[:, cols], op=ADD)
            nc.sync.dma_start(out=out_0[mt * P : (mt + 1) * P, cols], in_=y_tile[u][:])

        def round_y(u):
            if u < STAGE_UNITS or u == LAST_UNIT:
                return
            if u % STEP_UNITS in GPSIMD_UNITS or u == LAST_UNIT - 2:
                nc.gpsimd.tensor_scalar(
                    out=new_rounded(u), in0=by_half(y_tile[u][:]), scalar1=1.0, scalar2=0.0, op0=MULT, op1=ADD
                )
            else:
                nc.scalar.copy(out=new_rounded(u), in_=by_half(y_tile[u][:]))

        def turn(pair):
            bank = psum.tile([P, 2, 2, P], F32, name="bank", tag="bank%d" % (pair % STEP_PAIRS))
            for j in range(2):
                words = rounded[2 * pair + j][:].bitcast(F32)
                for h in range(2):
                    nc.tensor.transpose(bank[:, j, h, :], words[:, h * P : (h + 1) * P], ident[:])
            tag = "turned%d" % (pair % TURNED_BUFS)
            turned[pair] = ring.tile([P, 2 * W], BF16, name="turned", tag=tag, align_bytes=64)
            nc.scalar.copy(
                out=turned[pair][:].bitcast(F32).rearrange("p (j m h) -> p j m h", j=2, h=2),
                in_=bank[:].rearrange("p j h m -> p j m h"),
            )

        def quantize(pair):
            if 2 * pair < STAGE_UNITS:
                nc.vector.quantize_mx(
                    out=st_codes[pair][:].bitcast(FP8X4), scales=st_plane[pair][:], in_=turned[pair][:]
                )
                return
            mt, n = place(2 * pair)
            cols = slice(mt * P, (mt + 2) * P)
            nc.vector.quantize_mx(
                out=y_codes[n][:, cols].bitcast(FP8X4), scales=y_plane[n][:, cols], in_=turned[pair][:]
            )
            if mt + 2 in WORD_CUTS:
                lo, hi = P * WORD_CUTS[WORD_CUTS.index(mt + 2) - 1], P * (mt + 2)
                dst = out_1[n].rearrange("p m t -> p (m t)")
                nc.sync.dma_start(out=dst[:, 4 * lo : 4 * hi].bitcast(I32), in_=y_codes[n][:, lo:hi].bitcast(I32))
            if mt + 2 == TILES:
                for quad in range(4):
                    queue = nc.scalar if (pair == LAST_PAIR and quad % 2) else nc.sync
                    queue.dma_start(
                        out=out_2[n, 4 * quad : 4 * quad + 4, :].bitcast(I32),
                        in_=y_plane[n][32 * quad : 32 * quad + 4, :].bitcast(I32),
                    )

        quantize_after = {}
        for step in range(STEPS):
            first = STEP_UNITS * step
            last_step = step == STEPS - 1
            halves = [half for half in range(2 * PIECES) if HALF_STEPS * half // HALVES == step]
            pieces = [i for i in range(PIECES) if step == (i + 1 if i < PIECES - 2 else i)]
            pairs = list(range(STEP_PAIRS * max(step - 1, 0), STEP_PAIRS * step + last_step))
            early_halves = halves[:-1] or halves
            for half in early_halves:
                lay_out_a(half)
            for i in range(STEP_UNITS):
                u = first + i
                if i % 2 == 0 and i // 2 < len(pieces):
                    quantize_a(pieces[i // 2])
                multiply(u)
                add(u)
                if u in quantize_after:
                    quantize(quantize_after[u])
                if i != LEAD - 1:
                    round_y(u)
                elif last_step:
                    round_y(u)
                    for j, pair in enumerate(pairs):
                        turn(pair)
                        if j < 2:
                            quantize(pair)
                        else:
                            quantize_after[u + j - 1] = pair
                else:
                    if step == 0:
                        spread_bias()
                    for j, pair in enumerate(pairs):
                        turn(pair)
                        quantize_after[u + j + 1] = pair
                    round_y(u)
                    for half in halves[len(early_halves) :]:
                        lay_out_a(half)
        for pair in (LAST_PAIR - 1, LAST_PAIR):
            turn(pair)
            quantize(pair)
